import numpy as np
import ml_dtypes


def mxq(x, axis, fmt="e4m3"):
    dtype, down = {"e4m3": (ml_dtypes.float8_e4m3fn, 7), "e5m2": (ml_dtypes.float8_e5m2, 14)}[fmt]
    v = np.moveaxis(np.asarray(x, np.float32).astype(ml_dtypes.bfloat16).astype(np.float64), axis, -1)
    blocks = v.reshape(v.shape[:-1] + (-1, 32))
    amax = np.abs(blocks).max(-1, keepdims=True)
    byte = np.maximum(np.where(amax > 0, np.frexp(amax)[1] - 1 + 127, 0) - down, 1)
    scale = np.exp2(byte - 127.0)
    codes = (blocks / scale).astype(np.float32).astype(dtype).astype(np.float64)
    return np.moveaxis((codes * scale).reshape(v.shape), -1, axis)


WIDE = False


def mx_kscale(k):
    if not WIDE:
        return np.ones(k)
    levels = np.array([10, -10, 5, -5, 0])
    if k % 512:
        return np.exp2(np.random.permutation(np.resize(levels, k // 32))).repeat(32)
    a = np.empty((k // 512, 16))
    for p in range(k // 512):
        a[p, :8] = np.random.permutation(np.resize(levels, 8))
        for g in range(8):
            far = levels[np.abs(levels - a[p, g]) >= 10]
            a[p, g + 8] = far[np.random.randint(len(far))]
    return np.exp2(a.ravel()).repeat(32)


def f64(x):
    return np.asarray(x).astype(np.float64)


def striped8(idx):
    return np.asarray(idx).reshape(8, -1, 16).transpose(0, 2, 1).reshape(128, -1).astype(np.uint16)


def unstriped8(offs):
    return offs.reshape(8, 16, -1).transpose(0, 2, 1).reshape(8, -1).astype(np.int64)


def pick8(x, idx, run):
    r = np.arange(len(x))
    return x[r[:, None], idx[r % (8 * run) // run]]


E2M1 = np.array([0.0, 0.5, 1.0, 1.5, 2.0, 3.0, 4.0, 6.0, -0.0, -0.5, -1.0, -1.5, -2.0, -3.0, -4.0, -6.0])


def pack_weight(w, fmt):
    k, n = w.shape
    w = f64(np.asarray(w, np.float32).astype(ml_dtypes.bfloat16)).reshape(k // 32, 32, n)
    amax = np.abs(w).max(1)
    if fmt == "e4m3":
        byte = np.frexp(amax)[1] - 1 + 127 - 7
    else:
        mant, ex = np.frexp(amax / 6.0)
        byte = np.where(mant > 0.5, ex, ex - 1) + 127
    byte = np.clip(np.where(amax > 0, byte, 1), 1, 254)
    scaled = (w * np.exp2(127.0 - byte)[:, None, :]).reshape(k, n).astype(np.float32)
    by_word = np.ascontiguousarray(scaled.reshape(k // 512, 128, 4, n).transpose(0, 1, 3, 2))
    if fmt == "e4m3":
        words = by_word.astype(ml_dtypes.float8_e4m3fn).view(np.uint8)
    else:
        c = by_word.astype(ml_dtypes.float4_e2m1fn).view(np.uint8) & 0xF
        words = (c[..., 0::2] | (c[..., 1::2] << 4)).reshape(k // 512, 128, 2 * n)
    return np.ascontiguousarray(words), np.ascontiguousarray(byte.astype(np.uint8).reshape(k // 512, 16, n))


def unpack_weight(words, scales, fmt):
    g, _, n = scales.shape
    words = np.ascontiguousarray(words).reshape(g, 128, n, -1)
    if fmt == "e4m3":
        vals = words.view(ml_dtypes.float8_e4m3fn).astype(np.float64)
    else:
        nib = np.empty((g, 128, n, 4), np.uint8)
        nib[..., 0::2] = words & 0xF
        nib[..., 1::2] = words >> 4
        vals = E2M1[nib]
    vals = vals * np.repeat(np.exp2(scales.astype(np.float64) - 127.0), 8, axis=1)[..., None]
    return vals.transpose(0, 1, 3, 2).reshape(g * 512, n)


def sigmoid(v):
    return 1.0 / (1.0 + np.exp(-v))


def sgn(shape):
    return np.random.uniform(0.5, 2.0, shape) * np.where(np.random.standard_normal(shape) < 0, -1.0, 1.0)


D, T, U, I, Q = 512, 1024, 1024, 512, 128


def setup_inputs():
    n = np.random.standard_normal
    idx = np.stack([np.random.permutation(U)[:I] for _ in range(8)])
    idx2 = np.stack([np.random.permutation(T)[:I] for _ in range(8)])
    idx3 = np.stack([np.random.permutation(T)[:I] for _ in range(8)])
    idx4 = np.stack([np.random.permutation(U)[:I] for _ in range(8)])
    idx5 = np.stack([np.random.permutation(U)[:I] for _ in range(8)])
    fd = mx_kscale(D)
    cachep = pack_weight(n((D, T)) / fd[:, None], "e4m3")
    draftp = pack_weight(n((D, U)) / fd[:, None], "e2m1")
    return {
        "query": (n((D, Q)) * 1.0 / np.sqrt(D) * fd[:, None]).astype(np.float32),
        "cache_words": cachep[0],
        "cache_scales": cachep[1],
        "draft_words": draftp[0],
        "draft_scales": draftp[1],
        "thr": (np.random.uniform(-2.0, 2.0, (Q, 1))).astype(np.float32),
        "slope": (sgn((Q, 1))).astype(np.float32),
        "offs": striped8(idx),
        "offs2": striped8(idx2),
        "offs3": striped8(idx3),
        "offs4": striped8(idx4),
        "offs5": striped8(idx5),
    }


def reference(query, cache_words, cache_scales, draft_words, draft_scales, thr, slope, offs, offs2, offs3, offs4, offs5):
    idx = unstriped8(offs)
    idx2 = unstriped8(offs2)
    idx3 = unstriped8(offs3)
    idx4 = unstriped8(offs4)
    idx5 = unstriped8(offs5)
    cacheu = unpack_weight(cache_words, cache_scales, "e4m3")
    draftu = unpack_weight(draft_words, draft_scales, "e2m1")
    queryq = mxq(f64(query), 0, "e4m3")
    a = queryq.T @ cacheu
    b = queryq.T @ draftu
    s1 = sigmoid(pick8(b, idx, 16) * f64(slope) + f64(thr))
    kp = np.zeros((Q, T))
    kp[np.arange(Q)[:, None], idx2[np.arange(Q) % 128 // 16]] = s1
    aa = a * kp
    v = np.maximum(pick8(aa, idx3, 16), pick8(b, idx4, 16))
    f1 = np.zeros((Q, U))
    f1[np.arange(Q)[:, None], idx4[np.arange(Q) % 128 // 16]] = v
    bb = f1 - b
    y = pick8(bb, idx5, 16)
    return y

@@ -1,0 +1,133 @@
+from contextlib import ExitStack
+
+import concourse.mybir as mybir
+
+F32 = mybir.dt.float32
+BF16 = mybir.dt.bfloat16
+I32 = mybir.dt.int32
+U32 = mybir.dt.uint32
+U16 = mybir.dt.uint16
+U8 = mybir.dt.uint8
+FP8X4 = mybir.dt.float8_e4m3fn_x4
+FP4X4 = mybir.dt.float4_e2m1fn_x4
+ALU = mybir.AluOpType
+ACT = mybir.ActivationFunctionType
+
+P = 128
+PACK = 4
+D, T, U, I, Q = 512, 1024, 1024, 512, 128
+LIST_COLS = I // 16
+HALF = I // 2
+B_CHUNK = 256
+A_CHUNK = 512
+FLOPS = 2 * D * Q * (T + U)
+
+
+def tile_attend_softkeep_two_kernel(tc, query, cache_words, cache_scales, draft_words, draft_scales,
+                                     thr, slope, offs, offs2, offs3, offs4, offs5, out):
+    nc = tc.nc
+    with ExitStack() as ctx:
+        sb = ctx.enter_context(tc.tile_pool(name="sb", bufs=1))
+        psum = ctx.enter_context(tc.psum_pool(name="psum", bufs=1))
+
+        def load_list(name, src):
+            lst = sb.tile([P, LIST_COLS], U16, name=name)
+            nc.sync.dma_start(lst[:], src)
+            return lst
+
+        def load_scales(queue, plane, src):
+            for quad in range(4):
+                queue.dma_start(plane[32 * quad:32 * quad + 4, :].bitcast(I32),
+                                src[0, 4 * quad:4 * quad + 4, :].bitcast(I32))
+
+        def list_half(lst, h):
+            return lst[:, h * LIST_COLS // 2:(h + 1) * LIST_COLS // 2]
+
+        d_rows = sb.tile([P, 2 * U], U8, align_bytes=64)
+        d_plane = d_rows[:, 0:U]
+        c_plane = sb.tile([P, T], U8, align_bytes=64)
+        nc.vector.memset(d_plane.bitcast(I32), 0)
+
+        q_raw = sb.tile([P, PACK, Q], F32)
+        nc.sync.dma_start(q_raw[:], query.rearrange("(p j) q -> p j q", j=PACK))
+        nc.scalar.dma_start(d_rows[0:4, :].bitcast(I32).rearrange("r (g c) -> r g c", g=2),
+                            draft_scales[0, 0:8, :].bitcast(I32).rearrange("(g r) c -> r g c", g=2))
+        for quad in (2, 3):
+            nc.scalar.dma_start(d_rows[32 * quad:32 * quad + 4, 0:U].bitcast(I32),
+                                draft_scales[0, 4 * quad:4 * quad + 4, :].bitcast(I32))
+        l1 = load_list("l1", offs)
+        d_words = sb.tile([P, 2 * U], U8, align_bytes=64)
+        nc.sync.dma_start(d_words[:].bitcast(I32), draft_words[0].bitcast(I32))
+        thr_sb = sb.tile([P, 1], F32)
+        nc.sync.dma_start(thr_sb[:], thr)
+        slope_sb = sb.tile([P, 1], F32)
+        nc.sync.dma_start(slope_sb[:], slope)
+        l2 = load_list("l2", offs2)
+        l4 = load_list("l4", offs4)
+        nc.vector.memset(c_plane[:].bitcast(I32), 0)
+        c_words = sb.tile([P, T], U32, align_bytes=64)
+        nc.sync.dma_start(c_words[:].bitcast(I32),
+                          cache_words[0].rearrange("p n t -> p (n t)").bitcast(I32))
+        load_scales(nc.sync, c_plane, cache_scales)
+        l3 = load_list("l3", offs3)
+        l5 = load_list("l5", offs5)
+
+        kp = sb.tile([P, T], F32)
+        f1 = sb.tile([P, U], F32)
+        nc.vector.memset(kp[:], 0.0)
+        nc.vector.memset(f1[:], 0.0)
+
+        q_words = sb.tile([P, Q], U32, align_bytes=64)
+        q_plane = sb.tile([P, Q], U8, align_bytes=64)
+        q_bf = [sb.tile([P, Q // 2, PACK], BF16, name="q_bf%d" % h, align_bytes=64) for h in range(2)]
+        for h in range(2):
+            nc.vector.tensor_copy(out=q_bf[h][:].rearrange("p (c i) t -> p c t i", i=4),
+                                  in_=q_raw[:, :, h * Q // 2:(h + 1) * Q // 2].rearrange("p t (c i) -> p c t i", i=4))
+        nc.vector.tensor_copy(out=d_rows[32:36, 0:U].bitcast(I32), in_=d_rows[0:4, U:2 * U].bitcast(I32))
+        for h in range(2):
+            cols = slice(h * Q // 2, (h + 1) * Q // 2)
+            nc.vector.quantize_mx(out=q_words[:, cols].bitcast(FP8X4), scales=q_plane[:, cols],
+                                  in_=q_bf[h][:].rearrange("p q t -> p (q t)"))
+
+        b = sb.tile([P, U], F32)
+        for n0 in range(0, U, B_CHUNK):
+            b_ps = psum.tile([P, B_CHUNK], F32, name="b_ps%d" % n0)
+            nc.tensor.matmul_mx(out=b_ps[:], lhsT=q_words[:].bitcast(FP8X4), lhsT_scale=q_plane[:],
+                                rhs=d_words[:, 2 * n0:2 * (n0 + B_CHUNK)].bitcast(FP4X4),
+                                rhs_scale=d_rows[:, n0:n0 + B_CHUNK], start=True, stop=True)
+            nc.vector.tensor_copy(out=b[:, n0:n0 + B_CHUNK], in_=b_ps[:])
+
+        s1 = sb.tile([P, I], F32)
+        nc.scalar.activation(s1[:], b[:].indirect(l1[:]), ACT.Sigmoid, bias=thr_sb[:], scale=slope_sb[:])
+        nc.scalar.activation(kp[:].indirect(l2[:]), s1[:], ACT.Copy)
+
+        b4 = sb.tile([P, I], F32)
+        nc.vector.tensor_copy(out=b4[:], in_=b[:].indirect(l4[:]))
+
+        aa = sb.tile([P, T], F32)
+        for n0 in range(0, T, A_CHUNK):
+            a_ps = psum.tile([P, A_CHUNK], F32, name="a_ps%d" % n0)
+            nc.tensor.matmul_mx(out=a_ps[:], lhsT=q_words[:].bitcast(FP8X4), lhsT_scale=q_plane[:],
+                                rhs=c_words[:, n0:n0 + A_CHUNK].bitcast(FP8X4),
+                                rhs_scale=c_plane[:, n0:n0 + A_CHUNK], start=True, stop=True)
+            nc.vector.tensor_tensor(out=aa[:, n0:n0 + A_CHUNK], in0=a_ps[:], in1=kp[:, n0:n0 + A_CHUNK], op=ALU.mult)
+
+        for h in range(2):
+            a3 = sb.tile([P, HALF], F32, name="a3")
+            if h == 0:
+                nc.scalar.activation(a3[:], aa[:].indirect(list_half(l3, h)), ACT.Copy)
+            else:
+                nc.vector.tensor_copy(out=a3[:], in_=aa[:].indirect(list_half(l3, h)))
+            v = sb.tile([P, HALF], F32, name="v_%d" % h)
+            nc.vector.tensor_tensor(out=v[:], in0=a3[:], in1=b4[:, h * HALF:(h + 1) * HALF], op=ALU.max)
+            nc.scalar.activation(f1[:].indirect(list_half(l4, h)), v[:], ACT.Copy)
+
+        bb = sb.tile([P, U], F32)
+        nc.vector.tensor_tensor(out=bb[:], in0=f1[:], in1=b[:], op=ALU.subtract)
+
+        y0 = sb.tile([P, HALF], F32)
+        nc.vector.tensor_copy(out=y0[:], in_=bb[:].indirect(list_half(l5, 0)))
+        nc.sync.dma_start(out[:, 0:HALF], y0[:])
+        y1 = sb.tile([P, HALF], F32)
+        nc.scalar.activation(y1[:], bb[:].indirect(list_half(l5, 1)), ACT.Copy)
+        nc.scalar.dma_start(out[:, HALF:I], y1[:])

@@ -20,6 +20,7 @@ LIST_COLS = I // 16
 HALF = I // 2
 B_CHUNK = 256
 A_CHUNK = 512
+VEC_COLS = 688
 FLOPS = 2 * D * Q * (T + U)
 
 
@@ -44,9 +45,8 @@ def tile_attend_softkeep_two_kernel(tc, query, cache_words, cache_scales, draft_
             return lst[:, h * LIST_COLS // 2:(h + 1) * LIST_COLS // 2]
 
         d_rows = sb.tile([P, 2 * U], U8, align_bytes=64)
-        d_plane = d_rows[:, 0:U]
         c_plane = sb.tile([P, T], U8, align_bytes=64)
-        nc.vector.memset(d_plane.bitcast(I32), 0)
+        nc.vector.memset(d_rows[:, 0:U].bitcast(I32), 0)
 
         q_raw = sb.tile([P, PACK, Q], F32)
         nc.sync.dma_start(q_raw[:], query.rearrange("(p j) q -> p j q", j=PACK))
@@ -90,12 +90,14 @@ def tile_attend_softkeep_two_kernel(tc, query, cache_words, cache_scales, draft_
                                   in_=q_bf[h][:].rearrange("p q t -> p (q t)"))
 
         b = sb.tile([P, U], F32)
+        b_banks = []
         for n0 in range(0, U, B_CHUNK):
             b_ps = psum.tile([P, B_CHUNK], F32, name="b_ps%d" % n0)
             nc.tensor.matmul_mx(out=b_ps[:], lhsT=q_words[:].bitcast(FP8X4), lhsT_scale=q_plane[:],
                                 rhs=d_words[:, 2 * n0:2 * (n0 + B_CHUNK)].bitcast(FP4X4),
                                 rhs_scale=d_rows[:, n0:n0 + B_CHUNK], start=True, stop=True)
             nc.vector.tensor_copy(out=b[:, n0:n0 + B_CHUNK], in_=b_ps[:])
+            b_banks.append(b_ps)
 
         s1 = sb.tile([P, I], F32)
         nc.scalar.activation(s1[:], b[:].indirect(l1[:]), ACT.Sigmoid, bias=thr_sb[:], scale=slope_sb[:])
@@ -104,13 +106,18 @@ def tile_attend_softkeep_two_kernel(tc, query, cache_words, cache_scales, draft_
         b4 = sb.tile([P, I], F32)
         nc.vector.tensor_copy(out=b4[:], in_=b[:].indirect(l4[:]))
 
-        aa = sb.tile([P, T], F32)
+        a_banks = []
         for n0 in range(0, T, A_CHUNK):
             a_ps = psum.tile([P, A_CHUNK], F32, name="a_ps%d" % n0)
             nc.tensor.matmul_mx(out=a_ps[:], lhsT=q_words[:].bitcast(FP8X4), lhsT_scale=q_plane[:],
                                 rhs=c_words[:, n0:n0 + A_CHUNK].bitcast(FP8X4),
                                 rhs_scale=c_plane[:, n0:n0 + A_CHUNK], start=True, stop=True)
-            nc.vector.tensor_tensor(out=aa[:, n0:n0 + A_CHUNK], in0=a_ps[:], in1=kp[:, n0:n0 + A_CHUNK], op=ALU.mult)
+            a_banks.append(a_ps)
+
+        aa = sb.tile([P, T], F32)
+        for n0 in range(0, T, A_CHUNK):
+            nc.vector.tensor_tensor(out=aa[:, n0:n0 + A_CHUNK], in0=a_banks[n0 // A_CHUNK][:], in1=kp[:, n0:n0 + A_CHUNK],
+                                    op=ALU.mult)
 
         for h in range(2):
             a3 = sb.tile([P, HALF], F32, name="a3")
@@ -123,7 +130,11 @@ def tile_attend_softkeep_two_kernel(tc, query, cache_words, cache_scales, draft_
             nc.scalar.activation(f1[:].indirect(list_half(l4, h)), v[:], ACT.Copy)
 
         bb = sb.tile([P, U], F32)
-        nc.vector.tensor_tensor(out=bb[:], in0=f1[:], in1=b[:], op=ALU.subtract)
+        nc.gpsimd.tensor_tensor(out=bb[:, VEC_COLS:U], in0=f1[:, VEC_COLS:U], in1=b[:, VEC_COLS:U], op=ALU.subtract)
+        for n0 in range(0, VEC_COLS, B_CHUNK):
+            n1 = min(n0 + B_CHUNK, VEC_COLS)
+            nc.vector.tensor_tensor(out=bb[:, n0:n1], in0=f1[:, n0:n1], in1=b_banks[n0 // B_CHUNK][:, 0:n1 - n0],
+                                    op=ALU.subtract)
 
         y0 = sb.tile([P, HALF], F32)
         nc.vector.tensor_copy(out=y0[:], in_=bb[:].indirect(list_half(l5, 0)))

@@ -20,7 +20,7 @@ LIST_COLS = I // 16
 HALF = I // 2
 B_CHUNK = 256
 A_CHUNK = 512
-VEC_COLS = 688
+LEAD = 64
 FLOPS = 2 * D * Q * (T + U)
 
 
@@ -73,9 +73,7 @@ def tile_attend_softkeep_two_kernel(tc, query, cache_words, cache_scales, draft_
         l5 = load_list("l5", offs5)
 
         kp = sb.tile([P, T], F32)
-        f1 = sb.tile([P, U], F32)
         nc.vector.memset(kp[:], 0.0)
-        nc.vector.memset(f1[:], 0.0)
 
         q_words = sb.tile([P, Q], U32, align_bytes=64)
         q_plane = sb.tile([P, Q], U8, align_bytes=64)
@@ -90,14 +88,17 @@ def tile_attend_softkeep_two_kernel(tc, query, cache_words, cache_scales, draft_
                                   in_=q_bf[h][:].rearrange("p q t -> p (q t)"))
 
         b = sb.tile([P, U], F32)
-        b_banks = []
         for n0 in range(0, U, B_CHUNK):
             b_ps = psum.tile([P, B_CHUNK], F32, name="b_ps%d" % n0)
             nc.tensor.matmul_mx(out=b_ps[:], lhsT=q_words[:].bitcast(FP8X4), lhsT_scale=q_plane[:],
                                 rhs=d_words[:, 2 * n0:2 * (n0 + B_CHUNK)].bitcast(FP4X4),
                                 rhs_scale=d_rows[:, n0:n0 + B_CHUNK], start=True, stop=True)
             nc.vector.tensor_copy(out=b[:, n0:n0 + B_CHUNK], in_=b_ps[:])
-            b_banks.append(b_ps)
+
+        f1_hi = sb.tile([P, U], F32, name="d_words", align_bytes=64)
+        nc.vector.memset(f1_hi[:], 0.0)
+        f1_lo = sb.tile([P, U], F32, name="d_rows", align_bytes=64)
+        nc.vector.memset(f1_lo[:], 0.0)
 
         s1 = sb.tile([P, I], F32)
         nc.scalar.activation(s1[:], b[:].indirect(l1[:]), ACT.Sigmoid, bias=thr_sb[:], scale=slope_sb[:])
@@ -119,22 +120,23 @@ def tile_attend_softkeep_two_kernel(tc, query, cache_words, cache_scales, draft_
             nc.vector.tensor_tensor(out=aa[:, n0:n0 + A_CHUNK], in0=a_banks[n0 // A_CHUNK][:], in1=kp[:, n0:n0 + A_CHUNK],
                                     op=ALU.mult)
 
-        for h in range(2):
-            a3 = sb.tile([P, HALF], F32, name="a3")
-            if h == 0:
-                nc.scalar.activation(a3[:], aa[:].indirect(list_half(l3, h)), ACT.Copy)
-            else:
-                nc.vector.tensor_copy(out=a3[:], in_=aa[:].indirect(list_half(l3, h)))
-            v = sb.tile([P, HALF], F32, name="v_%d" % h)
-            nc.vector.tensor_tensor(out=v[:], in0=a3[:], in1=b4[:, h * HALF:(h + 1) * HALF], op=ALU.max)
-            nc.scalar.activation(f1[:].indirect(list_half(l4, h)), v[:], ACT.Copy)
+        v = sb.tile([P, I], F32)
 
+        def keep_larger(picked, i0, i1, window):
+            nc.vector.tensor_tensor(out=v[:, i0:i1], in0=picked, in1=b4[:, i0:i1], op=ALU.max)
+            nc.scalar.activation(window[:].indirect(l4[:, i0 // 16:i1 // 16]), v[:, i0:i1], ACT.Copy)
+
+        a3 = sb.tile([P, I - LEAD], F32)
+        nc.scalar.activation(a3[:, HALF - LEAD:I - LEAD], aa[:].indirect(list_half(l3, 0)), ACT.Copy)
+        keep_larger(a3[:, HALF - LEAD:HALF], 0, LEAD, f1_hi)
+        keep_larger(a3[:, HALF:I - LEAD], LEAD, HALF, f1_lo)
+        nc.vector.tensor_copy(out=a3[:, 0:HALF], in_=aa[:].indirect(list_half(l3, 1)))
+        keep_larger(a3[:, 0:HALF], HALF, I, f1_hi)
+
+        bb_lo = sb.tile([P, U], F32)
+        nc.vector.tensor_tensor(out=bb_lo[:], in0=f1_lo[:], in1=b[:], op=ALU.subtract)
         bb = sb.tile([P, U], F32)
-        nc.gpsimd.tensor_tensor(out=bb[:, VEC_COLS:U], in0=f1[:, VEC_COLS:U], in1=b[:, VEC_COLS:U], op=ALU.subtract)
-        for n0 in range(0, VEC_COLS, B_CHUNK):
-            n1 = min(n0 + B_CHUNK, VEC_COLS)
-            nc.vector.tensor_tensor(out=bb[:, n0:n1], in0=f1[:, n0:n1], in1=b_banks[n0 // B_CHUNK][:, 0:n1 - n0],
-                                    op=ALU.subtract)
+        nc.vector.tensor_tensor(out=bb[:], in0=f1_hi[:], in1=bb_lo[:], op=ALU.add)
 
         y0 = sb.tile([P, HALF], F32)
         nc.vector.tensor_copy(out=y0[:], in_=bb[:].indirect(list_half(l5, 0)))

from contextlib import ExitStack

import concourse.mybir as mybir

F32 = mybir.dt.float32
BF16 = mybir.dt.bfloat16
I32 = mybir.dt.int32
U32 = mybir.dt.uint32
U16 = mybir.dt.uint16
U8 = mybir.dt.uint8
FP8X4 = mybir.dt.float8_e4m3fn_x4
FP4X4 = mybir.dt.float4_e2m1fn_x4
ALU = mybir.AluOpType
ACT = mybir.ActivationFunctionType

P = 128
PACK = 4
D, T, U, I, Q = 512, 1024, 1024, 512, 128
LIST_COLS = I // 16
HALF = I // 2
B_CHUNK = 256
A_CHUNK = 512
LEAD = 64
FLOPS = 2 * D * Q * (T + U)


def tile_attend_softkeep_two_kernel(tc, query, cache_words, cache_scales, draft_words, draft_scales,
                                     thr, slope, offs, offs2, offs3, offs4, offs5, out):
    nc = tc.nc
    with ExitStack() as ctx:
        sb = ctx.enter_context(tc.tile_pool(name="sb", bufs=1))
        psum = ctx.enter_context(tc.psum_pool(name="psum", bufs=1))

        def load_list(name, src):
            lst = sb.tile([P, LIST_COLS], U16, name=name)
            nc.sync.dma_start(lst[:], src)
            return lst

        def load_scales(queue, plane, src):
            for quad in range(4):
                queue.dma_start(plane[32 * quad:32 * quad + 4, :].bitcast(I32),
                                src[0, 4 * quad:4 * quad + 4, :].bitcast(I32))

        def list_half(lst, h):
            return lst[:, h * LIST_COLS // 2:(h + 1) * LIST_COLS // 2]

        d_rows = sb.tile([P, 2 * U], U8, align_bytes=64)
        c_plane = sb.tile([P, T], U8, align_bytes=64)
        nc.vector.memset(d_rows[:, 0:U].bitcast(I32), 0)

        q_raw = sb.tile([P, PACK, Q], F32)
        nc.sync.dma_start(q_raw[:], query.rearrange("(p j) q -> p j q", j=PACK))
        nc.scalar.dma_start(d_rows[0:4, :].bitcast(I32).rearrange("r (g c) -> r g c", g=2),
                            draft_scales[0, 0:8, :].bitcast(I32).rearrange("(g r) c -> r g c", g=2))
        for quad in (2, 3):
            nc.scalar.dma_start(d_rows[32 * quad:32 * quad + 4, 0:U].bitcast(I32),
                                draft_scales[0, 4 * quad:4 * quad + 4, :].bitcast(I32))
        l1 = load_list("l1", offs)
        d_words = sb.tile([P, 2 * U], U8, align_bytes=64)
        nc.sync.dma_start(d_words[:].bitcast(I32), draft_words[0].bitcast(I32))
        thr_sb = sb.tile([P, 1], F32)
        nc.sync.dma_start(thr_sb[:], thr)
        slope_sb = sb.tile([P, 1], F32)
        nc.sync.dma_start(slope_sb[:], slope)
        l2 = load_list("l2", offs2)
        l4 = load_list("l4", offs4)
        nc.vector.memset(c_plane[:].bitcast(I32), 0)
        c_words = sb.tile([P, T], U32, align_bytes=64)
        nc.sync.dma_start(c_words[:].bitcast(I32),
                          cache_words[0].rearrange("p n t -> p (n t)").bitcast(I32))
        load_scales(nc.sync, c_plane, cache_scales)
        l3 = load_list("l3", offs3)
        l5 = load_list("l5", offs5)

        kp = sb.tile([P, T], F32)
        nc.vector.memset(kp[:], 0.0)

        q_words = sb.tile([P, Q], U32, align_bytes=64)
        q_plane = sb.tile([P, Q], U8, align_bytes=64)
        q_bf = [sb.tile([P, Q // 2, PACK], BF16, name="q_bf%d" % h, align_bytes=64) for h in range(2)]
        for h in range(2):
            nc.vector.tensor_copy(out=q_bf[h][:].rearrange("p (c i) t -> p c t i", i=4),
                                  in_=q_raw[:, :, h * Q // 2:(h + 1) * Q // 2].rearrange("p t (c i) -> p c t i", i=4))
        nc.vector.tensor_copy(out=d_rows[32:36, 0:U].bitcast(I32), in_=d_rows[0:4, U:2 * U].bitcast(I32))
        for h in range(2):
            cols = slice(h * Q // 2, (h + 1) * Q // 2)
            nc.vector.quantize_mx(out=q_words[:, cols].bitcast(FP8X4), scales=q_plane[:, cols],
                                  in_=q_bf[h][:].rearrange("p q t -> p (q t)"))

        b = sb.tile([P, U], F32)
        for n0 in range(0, U, B_CHUNK):
            b_ps = psum.tile([P, B_CHUNK], F32, name="b_ps%d" % n0)
            nc.tensor.matmul_mx(out=b_ps[:], lhsT=q_words[:].bitcast(FP8X4), lhsT_scale=q_plane[:],
                                rhs=d_words[:, 2 * n0:2 * (n0 + B_CHUNK)].bitcast(FP4X4),
                                rhs_scale=d_rows[:, n0:n0 + B_CHUNK], start=True, stop=True)
            nc.vector.tensor_copy(out=b[:, n0:n0 + B_CHUNK], in_=b_ps[:])

        f1_hi = sb.tile([P, U], F32, name="d_words", align_bytes=64)
        nc.vector.memset(f1_hi[:], 0.0)
        f1_lo = sb.tile([P, U], F32, name="d_rows", align_bytes=64)
        nc.vector.memset(f1_lo[:], 0.0)

        s1 = sb.tile([P, I], F32)
        nc.scalar.activation(s1[:], b[:].indirect(l1[:]), ACT.Sigmoid, bias=thr_sb[:], scale=slope_sb[:])
        nc.scalar.activation(kp[:].indirect(l2[:]), s1[:], ACT.Copy)

        b4 = sb.tile([P, I], F32)
        nc.vector.tensor_copy(out=b4[:], in_=b[:].indirect(l4[:]))

        a_banks = []
        for n0 in range(0, T, A_CHUNK):
            a_ps = psum.tile([P, A_CHUNK], F32, name="a_ps%d" % n0)
            nc.tensor.matmul_mx(out=a_ps[:], lhsT=q_words[:].bitcast(FP8X4), lhsT_scale=q_plane[:],
                                rhs=c_words[:, n0:n0 + A_CHUNK].bitcast(FP8X4),
                                rhs_scale=c_plane[:, n0:n0 + A_CHUNK], start=True, stop=True)
            a_banks.append(a_ps)

        aa = sb.tile([P, T], F32)
        for n0 in range(0, T, A_CHUNK):
            nc.vector.tensor_tensor(out=aa[:, n0:n0 + A_CHUNK], in0=a_banks[n0 // A_CHUNK][:], in1=kp[:, n0:n0 + A_CHUNK],
                                    op=ALU.mult)

        v = sb.tile([P, I], F32)

        def keep_larger(picked, i0, i1, window):
            nc.vector.tensor_tensor(out=v[:, i0:i1], in0=picked, in1=b4[:, i0:i1], op=ALU.max)
            nc.scalar.activation(window[:].indirect(l4[:, i0 // 16:i1 // 16]), v[:, i0:i1], ACT.Copy)

        a3 = sb.tile([P, I - LEAD], F32)
        nc.scalar.activation(a3[:, HALF - LEAD:I - LEAD], aa[:].indirect(list_half(l3, 0)), ACT.Copy)
        keep_larger(a3[:, HALF - LEAD:HALF], 0, LEAD, f1_hi)
        keep_larger(a3[:, HALF:I - LEAD], LEAD, HALF, f1_lo)
        nc.vector.tensor_copy(out=a3[:, 0:HALF], in_=aa[:].indirect(list_half(l3, 1)))
        keep_larger(a3[:, 0:HALF], HALF, I, f1_hi)

        bb_lo = sb.tile([P, U], F32)
        nc.vector.tensor_tensor(out=bb_lo[:], in0=f1_lo[:], in1=b[:], op=ALU.subtract)
        bb = sb.tile([P, U], F32)
        nc.vector.tensor_tensor(out=bb[:], in0=f1_hi[:], in1=bb_lo[:], op=ALU.add)

        y0 = sb.tile([P, HALF], F32)
        nc.vector.tensor_copy(out=y0[:], in_=bb[:].indirect(list_half(l5, 0)))
        nc.sync.dma_start(out[:, 0:HALF], y0[:])
        y1 = sb.tile([P, HALF], F32)
        nc.scalar.activation(y1[:], bb[:].indirect(list_half(l5, 1)), ACT.Copy)
        nc.scalar.dma_start(out[:, HALF:I], y1[:])
